import numpy as np, ml_dtypes
CORES = [3,11,19,27,35,43]
N = 6
import mx_ref
BF = ml_dtypes.bfloat16
def cols(t, e):
    v = np.concatenate([t.reshape(128, -1, 4), np.zeros((128, 1, 4), BF)], axis=1)
    return np.ascontiguousarray(v[:, e]).reshape(128, -1)
def f(rng, *shape):
    return mx_ref.flush((rng.standard_normal(shape, dtype=np.float32) * np.exp2(rng.integers(-2, 3, shape[:-1] + (1,)))).astype(BF))
def wide(rng, *shape, cols=0):
    v = rng.standard_normal(shape, dtype=np.float32) * np.exp2(rng.integers(-12, 13, shape)).astype(np.float32)
    if cols: v *= np.repeat(np.exp2(rng.integers(-cols, cols + 1, shape[:-2] + (1, shape[-1] // 4))) * (rng.random(shape[:-2] + (1, shape[-1] // 4)) > 0.0625), 4, axis=-1).astype(np.float32)
    return mx_ref.flush(v.astype(BF))
T, NBIT, K, O = 160, 8, 256, 3
def planes(rng):
    v = np.zeros((N, 128, 512), BF); v[:, :, :4 * NBIT] = f(rng, N, 128, 4 * NBIT); return v
def setup_inputs(rng):
    return {"x": f(rng, N, 128, 4 * T), "hp": planes(rng), "e": f(rng, N, 128, 4 * K), "qw": f(rng, N, 128, O * 512)}
def setup_inputs_zero(rng):
    d = setup_inputs(rng)
    for r in rng.permutation(N)[:N // 2]:
        i = rng.integers(0, NBIT); d["hp"][r, :, 4 * i:4 * i + 4] = 0
    for r in range(N):
        for j in rng.permutation(T)[:T // 8]: d["x"][r, :, 4 * j:4 * j + 4] = 0
    return d
def setup_inputs_onebucket(rng):
    d = setup_inputs(rng); d["x"] = np.tile(d["hp"][rng.integers(0, N)][:, :4], (N, 1, T)); return d
def setup_inputs_all(rng):
    d = setup_inputs(rng); g = f(rng, 128, 4).astype(np.float32)[None, :, None, :]
    d["hp"][:, :, :4 * NBIT] = (g * np.exp2(rng.integers(0, 4, (N, 1, NBIT, 1)))).reshape(N, 128, -1).astype(BF)
    s = np.stack([rng.permutation(T) % 2 * 2 - 1 for r in range(N)]) * np.exp2(rng.integers(0, 4, (N, T)))
    d["x"] = (g * s[:, None, :, None]).reshape(N, 128, -1).astype(BF); return d
def setup_inputs_small(rng):
    d = setup_inputs(rng)
    for k in ("x", "hp"):
        v = d[k].astype(np.float32) * np.float32(2.0 ** -24)
        d[k] = mx_ref.flush(np.where(np.abs(v) < np.float32(2.0 ** -30), np.float32(0), v).astype(BF))
    return d
def setup_inputs_spread(rng):
    d = setup_inputs(rng); d["x"] = wide(rng, N, 128, 4 * T, cols=8); d["e"] = wide(rng, N, 128, 4 * K, cols=8); return d
def check_inputs(d):
    b = []
    if (np.asarray(d["hp"]).astype(np.float32)[:, :, 4 * NBIT:] != 0).any(): b.append("hp")
    return b
def reference(x, hp, e, qw):
    X = [mx_ref.quantize(x[r]) for r in range(N)]
    H = [mx_ref.quantize(hp[q]) for q in range(N)]
    W = [[mx_ref.quantize(np.ascontiguousarray(qw[r][:, 512 * o:512 * o + 512])) for o in range(O)] for r in range(N)]
    y = np.zeros((N, 128, N * O * T), np.float32); bk = np.zeros((N, N, T), np.float32)
    for r in range(N):
        for q in range(N):
            s = mx_ref.matmul(H[q], X[r])
            b = np.zeros(T, int)
            for i in range(NBIT): b += 2 ** i * (s[i] > 0)
            bk[r, q] = b
            c = mx_ref.quantize(cols(e[q], b))
            for o in range(O):
                k = (q * O + o) * T
                y[r][:, k:k + T] = mx_ref.matmul(W[r][o], c)
    return {"y": y, "bk": bk}

@@ -1,0 +1,279 @@
+from concourse.bass import DstId, RemoteDMATransfer
+from concourse.mybir import dt, AluOpType, ActivationFunctionType
+
+N, TOK, NBIT, K, O = 6, 160, 8, 256, 3
+NC = TOK // 16
+NP = NBIT * N
+PB = 3
+PT = 5
+A0 = NBIT
+OWN = A0 + NBIT * (N - 1)
+
+SCRATCH = {
+    "hpt": ("sbuf", [128, 512], "bfloat16"),
+    "et": ("sbuf", [128, 4 * K], "bfloat16"),
+    "xs": ("sbuf", [128, NC, 64], "bfloat16"),
+    "xrep": ("sbuf", [128, NC, 512], "bfloat16"),
+    "qwt": ("sbuf", [128, O * 512], "bfloat16"),
+    "pc": ("sbuf", [128, OWN + 128], "float8_e4m3fn_x4"),
+    "pz": ("sbuf", [128, OWN + 128], "uint8"),
+    "ec": ("sbuf", [128, K], "float8_e4m3fn_x4"),
+    "ez": ("sbuf", [128, K], "uint8"),
+    "hc": ("sbuf", [128, K], "float8_e4m3fn_x4"),
+    "hz": ("sbuf", [128, K], "uint8"),
+    "xc": ("sbuf", [128, NC * 128], "float8_e4m3fn_x4"),
+    "xz": ("sbuf", [128, NC * 128], "uint8"),
+    "wc": ("sbuf", [128, O * 128], "float8_e4m3fn_x4"),
+    "wz": ("sbuf", [128, O * 128], "uint8"),
+    "coef": ("sbuf", [128, NC * NP], "float32"),
+    "bits": ("sbuf", [128, NC * NP], "float32"),
+    "sc": ("sbuf", [128, NC * NP], "float32"),
+    "li": ("sbuf", [128, NC * N], "uint16"),
+    "bf": ("sbuf", [128, 64], "float32"),
+    "bt": ("sbuf", [128, 64], "float32"),
+    "pr": ("sbuf", [128, N * O * K], "float32"),
+    "yo": ("sbuf", [128, N * O * TOK], "float32"),
+}
+for _j in range(N - 1):
+    SCRATCH["tc%d" % _j] = ("sbuf", [128, K], "float8_e4m3fn_x4")
+    SCRATCH["tz%d" % _j] = ("sbuf", [128, K], "uint8")
+for _j in range(PT):
+    SCRATCH["pt%d" % _j] = ("psum", [128, 512], "float32")
+for _j in range(PB):
+    SCRATCH["pb%d" % _j] = ("psum", [128, 512], "float32")
+
+SEMAPHORES = ["lde", "ldh", "ldx", "ldw", "sv", "ss", "st", "ls", "hpl", "hzs", "hcs", "pls", "yst"] + ["tb%d" % j for j in range(N)]
+
+
+def bits_of(engines):
+    return sum(1 << e for e in engines)
+
+
+def roads(R, T, topo):
+    me = T.rank_of(R)
+    far = sorted((c for c in T.cores if c != R), key=lambda c: (T.rank_of(c) - me) % N)
+    plane = [c for c in far if topo.same_plane(topo.chip(R), topo.chip(c))]
+    mate = [c for c in far if topo.mates(topo.chip(R), topo.chip(c))]
+    diag = [c for c in far if c not in plane and c not in mate]
+    others = [c for c in topo.cores_of(R) if c != R]
+    owners = [c for c in others if all(topo.may_write(c, d) for d in far)]
+    c1 = [c for c in owners if topo.die(c) == topo.die(R)][0]
+    c2 = [c for c in owners if topo.die(c) != topo.die(R)][0]
+    ha, hb = [c for c in others if c not in owners and topo.die(c) != topo.die(R)][:2]
+    return diag + mate + plane, c1, c2, ha, hb
+
+
+def dst(c, topo):
+    rid, pid, _ = topo.addr(c)
+    return DstId(rid=rid, pnc=pid)
+
+
+def copy_to(cores, src, dsts, mask, sem, topo):
+    return RemoteDMATransfer(dst_ids=[dst(c, topo) for c in cores], dma_engine_mask=mask, remote_sem=sem, srcs=[src], dsts=dsts)
+
+
+def helper_program(g, core, R, T, topo):
+    dests, c1, c2, ha, hb = roads(R, T, topo)
+    if core not in (c1, c2, ha, hb):
+        return
+    out = topo.engines(core, dests[-1])
+    mask, ne = bits_of(out), len(out)
+    nin = len(topo.engines(R, core))
+    codes = core in (c1, ha)
+    mine = [0, 1, 2] if core in (c1, c2) else [3, 4]
+    g.wait_ge(T.sem.hpl, nin)
+    if codes:
+        src = T.pc[:, OWN:OWN + NBIT].bitcast(dt.uint8)
+        ds = [T.pc[:, A0 + NBIT * j:A0 + NBIT * (j + 1)].bitcast(dt.uint8) for j in mine]
+    else:
+        src = T.pz[:, OWN:OWN + NBIT]
+        ds = [T.pz[:, A0 + NBIT * j:A0 + NBIT * (j + 1)] for j in mine]
+    g.remote_dma_fused([copy_to([dests[j] for j in mine], src, ds, mask, T.sem.pls, topo)], local_sem=T.sem.ls)
+    total = ne
+    if core in (ha, hb):
+        j = 3 if core == ha else 4
+        sem = T.sem["tb%d" % T.rank_of(R)]
+        rid, pid, _ = topo.addr(dests[j])
+        nt = len([e for e in topo.engines(R, core) if e not in topo.engines(R, dests[j])])
+        g.wait_ge(T.sem.hzs, nt)
+        g.remote_dma(T["tz%d" % j][:, 0:K], T.hz[:, 0:K], sem, T.sem.ls, pid, rid, mask)
+        g.wait_ge(T.sem.hcs, nt)
+        g.remote_dma(T["tc%d" % j][:, 0:K].bitcast(dt.uint8), T.hc[:, 0:K].bitcast(dt.uint8), sem, T.sem.ls, pid, rid, mask)
+        total += 2 * ne
+    g.wait_ge(T.sem.ls, total)
+
+
+def rank_program(g, core, T, topo):
+    rank = T.rank_of(core)
+    if rank is None:
+        for R in T.cores:
+            if topo.chip(R) == topo.chip(core):
+                helper_program(g, core, R, T, topo)
+        return
+    dests, c1, c2, ha, hb = roads(core, T, topo)
+    slot_q = [[T.rank_of(c) for c in T.cores if c != core and roads(c, T, topo)[0][j] == core][0] for j in range(N - 1)] + [rank]
+    on = topo.engines(core, ha)
+    off = topo.engines(core, dests[0])
+    inner = [e for e in on if e not in off]
+
+    queue = {"v": g.vector, "s": g.scalar, "t": g.tensor, "y": g.sync, "g": g}
+    own_sem = {"v": "sv", "s": "ss", "t": "st"}
+    count = {"v": 0, "s": 0, "t": 0}
+    seen = {}
+
+    def need(q, sem, val):
+        if seen.get((q, sem), 0) < val:
+            seen[(q, sem)] = val
+            queue[q].wait_ge(T.sem[sem], val)
+
+    def done(q, ins):
+        ins.then_inc(T.sem[own_sem[q]], 1)
+        count[q] += 1
+        return (own_sem[q], count[q])
+
+    COPY = ActivationFunctionType.Copy
+
+    def move(q, out, in_, after):
+        for s, v in after:
+            need(q, s, v)
+        if q == "v":
+            return done("v", g.vector.tensor_copy(out, in_))
+        return done("s", g.scalar.activation(out, in_, COPY))
+
+    g.sync.dma_start(T.et[:, :], T.e[:, :]).then_inc(T.sem.lde, 16)
+    g.scalar.dma_start(T.hpt[:, 0:4 * NBIT], T.hp[:, 0:4 * NBIT]).then_inc(T.sem.ldh, 16)
+    g.sync.dma_start(T.xs[:, :, :], T.x[:, :]).then_inc(T.sem.ldx, 16)
+    g.sync.dma_start(T.qwt[:, :], T.qw[:, :]).then_inc(T.sem.ldw, 16)
+
+    z = done("v", g.vector.memset(T.hpt[:, 4 * NBIT:512], 0.0))
+    half = done("v", g.vector.memset(T.coef[:, :], 0.5))
+    b0 = done("v", g.vector.memset(T.bf[:, :], 0.0))
+    need("v", "ldh", 16)
+    need("v", *z)
+    qh = done("v", g.vector.quantize_mx(T.pc[:, OWN:OWN + 128], T.pz[:, OWN:OWN + 128], T.hpt[:, :]))
+    need("v", *half)
+    half = done("v", g.vector.memset(T.coef[:, 0:NC * NP:NBIT], 0.0))
+    need("v", "lde", 16)
+    qe = done("v", g.vector.quantize_mx(T.ec[:, :], T.ez[:, :], T.et[:, :]))
+    cp = []
+    for k in range(8):
+        cp.append(move("s" if k < 3 else "v", T.xrep[:, :, 64 * k:64 * k + 64], T.xs[:, :, :], [("ldx", 16)]))
+    need("v", "ldw", 16)
+    qw = done("v", g.vector.quantize_mx(T.wc[:, :], T.wz[:, :], T.qwt[:, :]))
+    for s, v in (cp[2], cp[7]):
+        need("v", s, v)
+    qx = [done("v", g.vector.quantize_mx(T.xc[:, 128 * i:128 * i + 128], T.xz[:, 128 * i:128 * i + 128], T.xrep[:, i, :])) for i in range(NC)]
+
+    need("g", *qh)
+    pl = T.pc[:, OWN:OWN + NBIT].bitcast(dt.uint8)
+    g.remote_dma_fused([copy_to([c1, ha], pl, [pl, pl], bits_of(on), T.sem.hpl, topo)], local_sem=T.sem.ls)
+    pl = T.pz[:, OWN:OWN + NBIT]
+    g.remote_dma_fused([copy_to([c2, hb], pl, [pl, pl], bits_of(on), T.sem.hpl, topo)], local_sem=T.sem.ls)
+    need("g", *qe)
+    total = 2 * len(on)
+    for src, far, near, sem, codes in ((T.ez[:, 0:K], "tz", T.hz[:, 0:K], T.sem.hzs, False), (T.ec[:, 0:K], "tc", T.hc[:, 0:K], T.sem.hcs, True)):
+        fars = [T["%s%d" % (far, j)][:, 0:K] for j in range(3)]
+        if codes:
+            src, near, fars = src.bitcast(dt.uint8), near.bitcast(dt.uint8), [d.bitcast(dt.uint8) for d in fars]
+        g.remote_dma_fused([copy_to(dests[:3], src, fars, bits_of(off), T.sem["tb%d" % rank], topo),
+                            copy_to([ha, hb], src, [near, near], bits_of(inner), sem, topo)], local_sem=T.sem.ls)
+        total += len(on)
+
+    free = [None] * PT
+    unit = [0]
+
+    def products(cd, sc_, after):
+        res = []
+        for s, v in after:
+            need("t", s, v)
+        for o in range(O):
+            b = unit[0] % PT
+            unit[0] += 1
+            if free[b] is not None:
+                need("t", *free[b])
+            m = done("t", g.tensor.matmul_mx(T["pt%d" % b][:, 0:K], T.wc[:, 128 * o:128 * o + 128], T.wz[:, 128 * o:128 * o + 128],
+                                             cd[:, 0:K], sc_[:, 0:K], True, True))
+            res.append((b, m))
+        return res
+
+    def drain(q, slot, o, bm):
+        b, m = bm
+        a = (slot * O + o) * K
+        free[b] = move(q, T.pr[:, a:a + K], T["pt%d" % b][:, 0:K], [m])
+        return free[b]
+
+    def pick(q, slot, o, after):
+        r = slot_q[slot]
+        a, y = (slot * O + o) * K, (r * O + o) * TOK
+        return move(q, T.yo[:, y:y + TOK], T.pr[:, a:a + K].indirect(T.li[:, NC * r:NC * r + NC]), after)
+
+    def store(slot, o0, o1, after):
+        for s, v in after:
+            need("y", s, v)
+        y = (slot_q[slot] * O) * TOK
+        g.sync.dma_start(T.y[:, y + o0 * TOK:y + o1 * TOK], T.yo[:, y + o0 * TOK:y + o1 * TOK]).then_inc(T.sem.yst, 16)
+
+    own = N - 1
+    bm = products(T.ec, T.ez, [qe, qw])
+    dr_own = [drain("s", own, o, bm[o]) for o in range(O)]
+
+    need("t", "pls", 2 * len(off) * (N - 1))
+    bfree = [None] * PB
+    need("t", *qx[-1])
+    for i in range(NC):
+        b = i % PB
+        if bfree[b] is not None:
+            need("t", *bfree[b])
+        m = done("t", g.tensor.matmul_mx(T["pb%d" % b][:, 0:128], T.xc[:, 128 * i:128 * i + 128], T.xz[:, 128 * i:128 * i + 128],
+                                         T.pc[:, A0:A0 + 128], T.pz[:, A0:A0 + 128], True, True))
+        need("v", *m)
+        bfree[b] = done("v", g.vector.tensor_scalar(T.bits[:, NP * i:NP * i + NP], T["pb%d" % b][:, 0:NP], 0.0, 128.0, AluOpType.is_gt, AluOpType.mult))
+    need("v", *bfree[(NC - 1) % PB])
+    need("v", *half)
+    s = done("v", g.vector.tensor_tensor_scan(T.sc[:, :], T.coef[:, :], T.bits[:, :], 0.0, AluOpType.mult, AluOpType.add))
+    li = {}
+    for slot in [own] + list(range(N - 1)):
+        r = slot_q[slot]
+        li[slot] = move("v", T.li[:, NC * r:NC * r + NC], T.sc[:, NBIT * slot + NBIT - 1:NC * NP:NP], [s])
+
+    bm = products(T.tc0, T.tz0, [("tb%d" % slot_q[0], 2 * len(off))])
+    dr0 = [drain("s", 0, o, bm[o]) for o in range(O)]
+
+    def finish(slot, dr):
+        p0 = pick("v", slot, 0, [dr[0], li[slot]])
+        p1 = pick("s", slot, 1, [dr[1], li[slot]])
+        p2 = pick("v", slot, 2, [dr[2]])
+        store(slot, 0, O, [p0, p1, p2])
+
+    finish(own, dr_own)
+    finish(0, dr0)
+    need("v", *b0)
+    h = NC * N // 2
+    need("v", *li[N - 2])
+    move("v", T.bf[0:32, 0:h], T.li[0:32, 0:h], [])
+    f = move("v", T.bf[0:32, 32:32 + h], T.li[0:32, h:2 * h], [])
+    need("v", *f)
+    tr = done("v", g.vector.transpose(T.bt[0:32, :], T.bf[0:32, :]))
+    need("y", *tr)
+    g.sync.dma_start(T.bk[0:N // 2, :], T.bt[0:h, 0:16]).then_inc(T.sem.yst, 16)
+    g.sync.dma_start(T.bk[N // 2:N, :], T.bt[0:h, 32:48]).then_inc(T.sem.yst, 16)
+    nst = 4
+    for slot in range(1, N - 1):
+        bm = products(T["tc%d" % slot], T["tz%d" % slot], [("tb%d" % slot_q[slot], 2 * len(off))])
+        d0 = drain("v", slot, 0, bm[0])
+        d1 = drain("s", slot, 1, bm[1])
+        d2 = drain("s", slot, 2, bm[2])
+        p0 = pick("v", slot, 0, [d0])
+        p1 = pick("s", slot, 1, [d1, li[slot]])
+        p2 = pick("v", slot, 2, [d2])
+        if slot < N - 2:
+            store(slot, 0, O, [p0, p1, p2])
+            nst += 1
+        else:
+            store(slot, 0, 1, [p0])
+            store(slot, 1, O, [p1, p2])
+            nst += 2
+    need("y", "yst", 16 * nst)
+    need("g", "ls", total)
+    for q in ("v", "s", "t"):
+        need("g", own_sem[q], count[q])

@@ -3,20 +3,28 @@ from concourse.mybir import dt, AluOpType, ActivationFunctionType
 
 N, TOK, NBIT, K, O = 6, 160, 8, 256, 3
 NC = TOK // 16
-NP = NBIT * N
-PB = 3
-PT = 5
-A0 = NBIT
-OWN = A0 + NBIT * (N - 1)
+NR = NBIT * (N - 1)
+A0 = 128
+GAP = A0 + NR
+Z1 = GAP + NBIT
+ZL = 120
+GROUPS = ((0, 3), (3, 6), (6, 9), (9, 10))
+BANKS = 8
+SPLIT_LAST = True
 
 SCRATCH = {
-    "hpt": ("sbuf", [128, 512], "bfloat16"),
+    "hpt": ("sbuf", [128, 4 * (ZL + 128)], "bfloat16"),
+    "zt": ("sbuf", [128, 512], "bfloat16"),
     "et": ("sbuf", [128, 4 * K], "bfloat16"),
     "xs": ("sbuf", [128, NC, 64], "bfloat16"),
     "xrep": ("sbuf", [128, NC, 512], "bfloat16"),
     "qwt": ("sbuf", [128, O * 512], "bfloat16"),
-    "pc": ("sbuf", [128, OWN + 128], "float8_e4m3fn_x4"),
-    "pz": ("sbuf", [128, OWN + 128], "uint8"),
+    "hq": ("sbuf", [128, 128], "float8_e4m3fn_x4"),
+    "hqz": ("sbuf", [128, 128], "uint8"),
+    "pc": ("sbuf", [128, Z1 + 128], "float8_e4m3fn_x4"),
+    "pz": ("sbuf", [128, Z1 + 128], "uint8"),
+    "oc": ("sbuf", [128, ZL + 128], "float8_e4m3fn_x4"),
+    "oz": ("sbuf", [128, ZL + 128], "uint8"),
     "ec": ("sbuf", [128, K], "float8_e4m3fn_x4"),
     "ez": ("sbuf", [128, K], "uint8"),
     "hc": ("sbuf", [128, K], "float8_e4m3fn_x4"),
@@ -25,9 +33,11 @@ SCRATCH = {
     "xz": ("sbuf", [128, NC * 128], "uint8"),
     "wc": ("sbuf", [128, O * 128], "float8_e4m3fn_x4"),
     "wz": ("sbuf", [128, O * 128], "uint8"),
-    "coef": ("sbuf", [128, NC * NP], "float32"),
-    "bits": ("sbuf", [128, NC * NP], "float32"),
-    "sc": ("sbuf", [128, NC * NP], "float32"),
+    "coef": ("sbuf", [128, 3 * NR], "float32"),
+    "obits": ("sbuf", [128, NC * NBIT], "float32"),
+    "osc": ("sbuf", [128, NC * NBIT], "float32"),
+    "bits": ("sbuf", [128, NC * NR], "float32"),
+    "sc": ("sbuf", [128, NC * NR], "float32"),
     "li": ("sbuf", [128, NC * N], "uint16"),
     "bf": ("sbuf", [128, 64], "float32"),
     "bt": ("sbuf", [128, 64], "float32"),
@@ -37,12 +47,10 @@ SCRATCH = {
 for _j in range(N - 1):
     SCRATCH["tc%d" % _j] = ("sbuf", [128, K], "float8_e4m3fn_x4")
     SCRATCH["tz%d" % _j] = ("sbuf", [128, K], "uint8")
-for _j in range(PT):
-    SCRATCH["pt%d" % _j] = ("psum", [128, 512], "float32")
-for _j in range(PB):
+for _j in range(BANKS):
     SCRATCH["pb%d" % _j] = ("psum", [128, 512], "float32")
 
-SEMAPHORES = ["lde", "ldh", "ldx", "ldw", "sv", "ss", "st", "ls", "hpl", "hzs", "hcs", "pls", "yst"] + ["tb%d" % j for j in range(N)]
+SEMAPHORES = ["lde", "ldh", "ldx", "ldw", "gap", "sv", "ss", "st", "ls", "hpl", "hzs", "hcs", "pls", "yst"] + ["tb%d" % j for j in range(N)]
 
 
 def bits_of(engines):
@@ -72,21 +80,26 @@ def copy_to(cores, src, dsts, mask, sem, topo):
     return RemoteDMATransfer(dst_ids=[dst(c, topo) for c in cores], dma_engine_mask=mask, remote_sem=sem, srcs=[src], dsts=dsts)
 
 
+def engine_sets(R, near, far, topo):
+    off = topo.engines(R, far)
+    return off, [e for e in topo.engines(R, near) if e not in off]
+
+
 def helper_program(g, core, R, T, topo):
     dests, c1, c2, ha, hb = roads(R, T, topo)
     if core not in (c1, c2, ha, hb):
         return
     out = topo.engines(core, dests[-1])
     mask, ne = bits_of(out), len(out)
-    nin = len(topo.engines(R, core))
+    off, inner = engine_sets(R, core, dests[0], topo)
     codes = core in (c1, ha)
     mine = [0, 1, 2] if core in (c1, c2) else [3, 4]
-    g.wait_ge(T.sem.hpl, nin)
+    g.wait_ge(T.sem.hpl, len(off) if codes else len(inner))
     if codes:
-        src = T.pc[:, OWN:OWN + NBIT].bitcast(dt.uint8)
+        src = T.hq[:, 0:NBIT].bitcast(dt.uint8)
         ds = [T.pc[:, A0 + NBIT * j:A0 + NBIT * (j + 1)].bitcast(dt.uint8) for j in mine]
     else:
-        src = T.pz[:, OWN:OWN + NBIT]
+        src = T.hqz[:, 0:NBIT]
         ds = [T.pz[:, A0 + NBIT * j:A0 + NBIT * (j + 1)] for j in mine]
     g.remote_dma_fused([copy_to([dests[j] for j in mine], src, ds, mask, T.sem.pls, topo)], local_sem=T.sem.ls)
     total = ne
@@ -94,10 +107,9 @@ def helper_program(g, core, R, T, topo):
         j = 3 if core == ha else 4
         sem = T.sem["tb%d" % T.rank_of(R)]
         rid, pid, _ = topo.addr(dests[j])
-        nt = len([e for e in topo.engines(R, core) if e not in topo.engines(R, dests[j])])
-        g.wait_ge(T.sem.hzs, nt)
+        g.wait_ge(T.sem.hzs, len(inner))
         g.remote_dma(T["tz%d" % j][:, 0:K], T.hz[:, 0:K], sem, T.sem.ls, pid, rid, mask)
-        g.wait_ge(T.sem.hcs, nt)
+        g.wait_ge(T.sem.hcs, len(inner))
         g.remote_dma(T["tc%d" % j][:, 0:K].bitcast(dt.uint8), T.hc[:, 0:K].bitcast(dt.uint8), sem, T.sem.ls, pid, rid, mask)
         total += 2 * ne
     g.wait_ge(T.sem.ls, total)
@@ -112,9 +124,7 @@ def rank_program(g, core, T, topo):
         return
     dests, c1, c2, ha, hb = roads(core, T, topo)
     slot_q = [[T.rank_of(c) for c in T.cores if c != core and roads(c, T, topo)[0][j] == core][0] for j in range(N - 1)] + [rank]
-    on = topo.engines(core, ha)
-    off = topo.engines(core, dests[0])
-    inner = [e for e in on if e not in off]
+    off, inner = engine_sets(core, ha, dests[0], topo)
 
     queue = {"v": g.vector, "s": g.scalar, "t": g.tensor, "y": g.sync, "g": g}
     own_sem = {"v": "sv", "s": "ss", "t": "st"}
@@ -140,58 +150,68 @@ def rank_program(g, core, T, topo):
             return done("v", g.vector.tensor_copy(out, in_))
         return done("s", g.scalar.activation(out, in_, COPY))
 
+    def quantise(out, scales, in_, after):
+        for s, v in after:
+            need("v", s, v)
+        return done("v", g.vector.quantize_mx(out, scales, in_))
+
+    g.sync.dma_start(T.hpt[:, 4 * ZL:4 * (ZL + NBIT)], T.hp[:, 0:4 * NBIT]).then_inc(T.sem.ldh, 16)
     g.sync.dma_start(T.et[:, :], T.e[:, :]).then_inc(T.sem.lde, 16)
-    g.scalar.dma_start(T.hpt[:, 0:4 * NBIT], T.hp[:, 0:4 * NBIT]).then_inc(T.sem.ldh, 16)
     g.sync.dma_start(T.xs[:, :, :], T.x[:, :]).then_inc(T.sem.ldx, 16)
     g.sync.dma_start(T.qwt[:, :], T.qw[:, :]).then_inc(T.sem.ldw, 16)
 
-    z = done("v", g.vector.memset(T.hpt[:, 4 * NBIT:512], 0.0))
+    z = done("v", g.vector.memset(T.hpt[:, 4 * (ZL + NBIT):4 * (ZL + 128)], 0.0))
     half = done("v", g.vector.memset(T.coef[:, :], 0.5))
     b0 = done("v", g.vector.memset(T.bf[:, :], 0.0))
-    need("v", "ldh", 16)
-    need("v", *z)
-    qh = done("v", g.vector.quantize_mx(T.pc[:, OWN:OWN + 128], T.pz[:, OWN:OWN + 128], T.hpt[:, :]))
-    need("v", *half)
-    half = done("v", g.vector.memset(T.coef[:, 0:NC * NP:NBIT], 0.0))
-    need("v", "lde", 16)
-    qe = done("v", g.vector.quantize_mx(T.ec[:, :], T.ez[:, :], T.et[:, :]))
+    done("v", g.vector.memset(T.hpt[:, 0:4 * ZL], 0.0))
+    zz = done("v", g.vector.memset(T.zt[:, :], 0.0))
+    qh = quantise(T.hq[:, :], T.hqz[:, :], T.hpt[:, 4 * ZL:4 * (ZL + 128)], [("ldh", 16), z])
+    quantise(T.pc[:, 0:A0], T.pz[:, 0:A0], T.zt[:, :], [zz])
+    quantise(T.pc[:, Z1:Z1 + 128], T.pz[:, Z1:Z1 + 128], T.zt[:, :], [])
+    quantise(T.oc[:, :], T.oz[:, :], T.hpt[:, :], [])
+    half = done("v", g.vector.memset(T.coef[:, 0:3 * NR:NBIT], 0.0))
+    qe = quantise(T.ec[:, :], T.ez[:, :], T.et[:, :], [("lde", 16)])
     cp = []
     for k in range(8):
         cp.append(move("s" if k < 3 else "v", T.xrep[:, :, 64 * k:64 * k + 64], T.xs[:, :, :], [("ldx", 16)]))
-    need("v", "ldw", 16)
-    qw = done("v", g.vector.quantize_mx(T.wc[:, :], T.wz[:, :], T.qwt[:, :]))
-    for s, v in (cp[2], cp[7]):
-        need("v", s, v)
-    qx = [done("v", g.vector.quantize_mx(T.xc[:, 128 * i:128 * i + 128], T.xz[:, 128 * i:128 * i + 128], T.xrep[:, i, :])) for i in range(NC)]
+    qw = quantise(T.wc[:, :], T.wz[:, :], T.qwt[:, :], [("ldw", 16)])
+    qx = [quantise(T.xc[:, 128 * i:128 * i + 128], T.xz[:, 128 * i:128 * i + 128], T.xrep[:, i, :], [cp[2], cp[7]]) for i in range(NC)]
+    need("y", *qh)
+    g.sync.dma_start(T.pc[:, GAP:Z1].bitcast(dt.uint8), T.hq[:, NBIT:2 * NBIT].bitcast(dt.uint8)).then_inc(T.sem.gap, 16)
+    g.sync.dma_start(T.pz[:, GAP:Z1], T.hqz[:, NBIT:2 * NBIT]).then_inc(T.sem.gap, 16)
 
     need("g", *qh)
-    pl = T.pc[:, OWN:OWN + NBIT].bitcast(dt.uint8)
-    g.remote_dma_fused([copy_to([c1, ha], pl, [pl, pl], bits_of(on), T.sem.hpl, topo)], local_sem=T.sem.ls)
-    pl = T.pz[:, OWN:OWN + NBIT]
-    g.remote_dma_fused([copy_to([c2, hb], pl, [pl, pl], bits_of(on), T.sem.hpl, topo)], local_sem=T.sem.ls)
+    pl = T.hq[:, 0:NBIT].bitcast(dt.uint8)
+    g.remote_dma_fused([copy_to([c1, ha], pl, [pl, pl], bits_of(off), T.sem.hpl, topo)], local_sem=T.sem.ls)
+    pl = T.hqz[:, 0:NBIT]
+    g.remote_dma_fused([copy_to([c2, hb], pl, [pl, pl], bits_of(inner), T.sem.hpl, topo)], local_sem=T.sem.ls)
     need("g", *qe)
-    total = 2 * len(on)
+    total = len(off) + len(inner)
     for src, far, near, sem, codes in ((T.ez[:, 0:K], "tz", T.hz[:, 0:K], T.sem.hzs, False), (T.ec[:, 0:K], "tc", T.hc[:, 0:K], T.sem.hcs, True)):
         fars = [T["%s%d" % (far, j)][:, 0:K] for j in range(3)]
         if codes:
             src, near, fars = src.bitcast(dt.uint8), near.bitcast(dt.uint8), [d.bitcast(dt.uint8) for d in fars]
         g.remote_dma_fused([copy_to(dests[:3], src, fars, bits_of(off), T.sem["tb%d" % rank], topo),
                             copy_to([ha, hb], src, [near, near], bits_of(inner), sem, topo)], local_sem=T.sem.ls)
-        total += len(on)
+        total += len(off) + len(inner)
 
-    free = [None] * PT
+    free = [None] * BANKS
     unit = [0]
+
+    def bank():
+        b = unit[0] % BANKS
+        unit[0] += 1
+        if free[b] is not None:
+            need("t", *free[b])
+        return b
 
     def products(cd, sc_, after):
         res = []
         for s, v in after:
             need("t", s, v)
         for o in range(O):
-            b = unit[0] % PT
-            unit[0] += 1
-            if free[b] is not None:
-                need("t", *free[b])
-            m = done("t", g.tensor.matmul_mx(T["pt%d" % b][:, 0:K], T.wc[:, 128 * o:128 * o + 128], T.wz[:, 128 * o:128 * o + 128],
+            b = bank()
+            m = done("t", g.tensor.matmul_mx(T["pb%d" % b][:, 0:K], T.wc[:, 128 * o:128 * o + 128], T.wz[:, 128 * o:128 * o + 128],
                                              cd[:, 0:K], sc_[:, 0:K], True, True))
             res.append((b, m))
         return res
@@ -199,7 +219,7 @@ def rank_program(g, core, T, topo):
     def drain(q, slot, o, bm):
         b, m = bm
         a = (slot * O + o) * K
-        free[b] = move(q, T.pr[:, a:a + K], T["pt%d" % b][:, 0:K], [m])
+        free[b] = move(q, T.pr[:, a:a + K], T["pb%d" % b][:, 0:K], [m])
         return free[b]
 
     def pick(q, slot, o, after):
@@ -207,73 +227,93 @@ def rank_program(g, core, T, topo):
         a, y = (slot * O + o) * K, (r * O + o) * TOK
         return move(q, T.yo[:, y:y + TOK], T.pr[:, a:a + K].indirect(T.li[:, NC * r:NC * r + NC]), after)
 
-    def store(slot, o0, o1, after):
+    nst = [0]
+
+    def keep(out, in_, after):
         for s, v in after:
             need("y", s, v)
+        g.sync.dma_start(out, in_).then_inc(T.sem.yst, 16)
+        nst[0] += 1
+
+    def store(slot, o0, o1, after):
         y = (slot_q[slot] * O) * TOK
-        g.sync.dma_start(T.y[:, y + o0 * TOK:y + o1 * TOK], T.yo[:, y + o0 * TOK:y + o1 * TOK]).then_inc(T.sem.yst, 16)
+        keep(T.y[:, y + o0 * TOK:y + o1 * TOK], T.yo[:, y + o0 * TOK:y + o1 * TOK], after)
+
+    def bucket_products(lo, hi, cd, sc_, at, step):
+        b = bank()
+        for i in range(lo, hi):
+            a = at - step * (i - lo)
+            m = done("t", g.tensor.matmul_mx(T["pb%d" % b][:, 0:128], T.xc[:, 128 * i:128 * i + 128], T.xz[:, 128 * i:128 * i + 128],
+                                             cd[:, a:a + 128], sc_[:, a:a + 128], i == lo, i == hi - 1))
+        return b, m
+
+    def numbers(bm, bits, out, n):
+        b, m = bm
+        need("v", *m)
+        free[b] = done("v", g.vector.tensor_scalar(bits, T["pb%d" % b][:, 0:n], 0.0, 128.0, AluOpType.is_gt, AluOpType.mult))
+        need("v", *free[b])
+        need("v", *half)
+        return done("v", g.vector.tensor_tensor_scan(out, T.coef[:, 0:n], bits, 0.0, AluOpType.mult, AluOpType.add))
 
     own = N - 1
     bm = products(T.ec, T.ez, [qe, qw])
-    dr_own = [drain("s", own, o, bm[o]) for o in range(O)]
-
-    need("t", "pls", 2 * len(off) * (N - 1))
-    bfree = [None] * PB
+    dr = [drain("s", own, o, bm[o]) for o in range(O)]
     need("t", *qx[-1])
-    for i in range(NC):
-        b = i % PB
-        if bfree[b] is not None:
-            need("t", *bfree[b])
-        m = done("t", g.tensor.matmul_mx(T["pb%d" % b][:, 0:128], T.xc[:, 128 * i:128 * i + 128], T.xz[:, 128 * i:128 * i + 128],
-                                         T.pc[:, A0:A0 + 128], T.pz[:, A0:A0 + 128], True, True))
-        need("v", *m)
-        bfree[b] = done("v", g.vector.tensor_scalar(T.bits[:, NP * i:NP * i + NP], T["pb%d" % b][:, 0:NP], 0.0, 128.0, AluOpType.is_gt, AluOpType.mult))
-    need("v", *bfree[(NC - 1) % PB])
-    need("v", *half)
-    s = done("v", g.vector.tensor_tensor_scan(T.sc[:, :], T.coef[:, :], T.bits[:, :], 0.0, AluOpType.mult, AluOpType.add))
-    li = {}
-    for slot in [own] + list(range(N - 1)):
+    s = numbers(bucket_products(0, NC, T.oc, T.oz, ZL, NBIT), T.obits[:, :], T.osc[:, :], NC * NBIT)
+    li = {own: move("v", T.li[:, NC * rank:NC * rank + NC], T.osc[:, NBIT - 1:NC * NBIT:NBIT], [s])}
+    store(own, 0, O, [pick("s", own, o, [dr[o], li[own]]) for o in range(O)])
+
+    need("t", "gap", 32)
+    need("t", "pls", 2 * len(off) * (N - 1))
+    groups = [bucket_products(lo, hi, T.pc, T.pz, A0, NR) for lo, hi in GROUPS]
+    scans = [numbers(groups[k], T.bits[:, NR * lo:NR * hi], T.sc[:, NR * lo:NR * hi], NR * (hi - lo)) for k, (lo, hi) in enumerate(GROUPS)]
+
+    def make_list(slot):
         r = slot_q[slot]
-        li[slot] = move("v", T.li[:, NC * r:NC * r + NC], T.sc[:, NBIT * slot + NBIT - 1:NC * NP:NP], [s])
+        li[slot] = move("v", T.li[:, NC * r:NC * r + NC], T.sc[:, NBIT * slot + NBIT - 1:NC * NR:NR], [scans[-1]])
 
-    bm = products(T.tc0, T.tz0, [("tb%d" % slot_q[0], 2 * len(off))])
-    dr0 = [drain("s", 0, o, bm[o]) for o in range(O)]
+    pm, dr = {}, {}
 
-    def finish(slot, dr):
-        p0 = pick("v", slot, 0, [dr[0], li[slot]])
-        p1 = pick("s", slot, 1, [dr[1], li[slot]])
-        p2 = pick("v", slot, 2, [dr[2]])
-        store(slot, 0, O, [p0, p1, p2])
+    def fetch(slot):
+        pm[slot] = products(T["tc%d" % slot], T["tz%d" % slot], [("tb%d" % slot_q[slot], 2 * len(off))])
 
-    finish(own, dr_own)
-    finish(0, dr0)
+    make_list(0)
+    make_list(1)
+    fetch(0)
+    for o in range(O):
+        dr[0, o] = drain("s", 0, o, pm[0][o])
+    last = N - 2
+    for slot in range(N - 1):
+        nxt = slot + 1
+        if nxt <= last:
+            fetch(nxt)
+        p0 = pick("v", slot, 0, [dr[slot, 0], li[slot]])
+        if nxt <= last:
+            dr[nxt, 0] = drain("v", nxt, 0, pm[nxt][0])
+        p1 = pick("s", slot, 1, [dr[slot, 1], li[slot]])
+        if nxt <= last:
+            dr[nxt, 1] = drain("s", nxt, 1, pm[nxt][1])
+        p2 = pick("v", slot, 2, [dr[slot, 2]])
+        if nxt <= last:
+            dr[nxt, 2] = drain("s", nxt, 2, pm[nxt][2])
+        if slot < last:
+            if nxt < last:
+                make_list(nxt + 1)
+            store(slot, 0, O, [p0, p1, p2])
+        else:
+            store(slot, 0, 2, [p0, p1])
+            store(slot, 2, O, [p2])
+
     need("v", *b0)
     h = NC * N // 2
-    need("v", *li[N - 2])
-    move("v", T.bf[0:32, 0:h], T.li[0:32, 0:h], [])
+    move("v", T.bf[0:32, 0:h], T.li[0:32, 0:h], [li[N - 2]])
     f = move("v", T.bf[0:32, 32:32 + h], T.li[0:32, h:2 * h], [])
     need("v", *f)
     tr = done("v", g.vector.transpose(T.bt[0:32, :], T.bf[0:32, :]))
-    need("y", *tr)
-    g.sync.dma_start(T.bk[0:N // 2, :], T.bt[0:h, 0:16]).then_inc(T.sem.yst, 16)
-    g.sync.dma_start(T.bk[N // 2:N, :], T.bt[0:h, 32:48]).then_inc(T.sem.yst, 16)
-    nst = 4
-    for slot in range(1, N - 1):
-        bm = products(T["tc%d" % slot], T["tz%d" % slot], [("tb%d" % slot_q[slot], 2 * len(off))])
-        d0 = drain("v", slot, 0, bm[0])
-        d1 = drain("s", slot, 1, bm[1])
-        d2 = drain("s", slot, 2, bm[2])
-        p0 = pick("v", slot, 0, [d0])
-        p1 = pick("s", slot, 1, [d1, li[slot]])
-        p2 = pick("v", slot, 2, [d2])
-        if slot < N - 2:
-            store(slot, 0, O, [p0, p1, p2])
-            nst += 1
-        else:
-            store(slot, 0, 1, [p0])
-            store(slot, 1, O, [p1, p2])
-            nst += 2
-    need("y", "yst", 16 * nst)
+    keep(T.bk[0:N // 2, :], T.bt[0:h, 0:16], [tr])
+    keep(T.bk[N // 2:N, :], T.bt[0:h, 32:48], [])
+
+    need("y", "yst", 16 * nst[0])
     need("g", "ls", total)
     for q in ("v", "s", "t"):
         need("g", own_sem[q], count[q])

from concourse.bass import DstId, RemoteDMATransfer
from concourse.mybir import dt, AluOpType, ActivationFunctionType

N, TOK, NBIT, K, O = 6, 160, 8, 256, 3
NC = TOK // 16
NR = NBIT * (N - 1)
A0 = 128
GAP = A0 + NR
Z1 = GAP + NBIT
ZL = 120
GROUPS = ((0, 3), (3, 6), (6, 9), (9, 10))
BANKS = 8
SPLIT_LAST = True

SCRATCH = {
    "hpt": ("sbuf", [128, 4 * (ZL + 128)], "bfloat16"),
    "zt": ("sbuf", [128, 512], "bfloat16"),
    "et": ("sbuf", [128, 4 * K], "bfloat16"),
    "xs": ("sbuf", [128, NC, 64], "bfloat16"),
    "xrep": ("sbuf", [128, NC, 512], "bfloat16"),
    "qwt": ("sbuf", [128, O * 512], "bfloat16"),
    "hq": ("sbuf", [128, 128], "float8_e4m3fn_x4"),
    "hqz": ("sbuf", [128, 128], "uint8"),
    "pc": ("sbuf", [128, Z1 + 128], "float8_e4m3fn_x4"),
    "pz": ("sbuf", [128, Z1 + 128], "uint8"),
    "oc": ("sbuf", [128, ZL + 128], "float8_e4m3fn_x4"),
    "oz": ("sbuf", [128, ZL + 128], "uint8"),
    "ec": ("sbuf", [128, K], "float8_e4m3fn_x4"),
    "ez": ("sbuf", [128, K], "uint8"),
    "hc": ("sbuf", [128, K], "float8_e4m3fn_x4"),
    "hz": ("sbuf", [128, K], "uint8"),
    "xc": ("sbuf", [128, NC * 128], "float8_e4m3fn_x4"),
    "xz": ("sbuf", [128, NC * 128], "uint8"),
    "wc": ("sbuf", [128, O * 128], "float8_e4m3fn_x4"),
    "wz": ("sbuf", [128, O * 128], "uint8"),
    "coef": ("sbuf", [128, 3 * NR], "float32"),
    "obits": ("sbuf", [128, NC * NBIT], "float32"),
    "osc": ("sbuf", [128, NC * NBIT], "float32"),
    "bits": ("sbuf", [128, NC * NR], "float32"),
    "sc": ("sbuf", [128, NC * NR], "float32"),
    "li": ("sbuf", [128, NC * N], "uint16"),
    "bf": ("sbuf", [128, 64], "float32"),
    "bt": ("sbuf", [128, 64], "float32"),
    "pr": ("sbuf", [128, N * O * K], "float32"),
    "yo": ("sbuf", [128, N * O * TOK], "float32"),
}
for _j in range(N - 1):
    SCRATCH["tc%d" % _j] = ("sbuf", [128, K], "float8_e4m3fn_x4")
    SCRATCH["tz%d" % _j] = ("sbuf", [128, K], "uint8")
for _j in range(BANKS):
    SCRATCH["pb%d" % _j] = ("psum", [128, 512], "float32")

SEMAPHORES = ["lde", "ldh", "ldx", "ldw", "gap", "sv", "ss", "st", "ls", "hpl", "hzs", "hcs", "pls", "yst"] + ["tb%d" % j for j in range(N)]


def bits_of(engines):
    return sum(1 << e for e in engines)


def roads(R, T, topo):
    me = T.rank_of(R)
    far = sorted((c for c in T.cores if c != R), key=lambda c: (T.rank_of(c) - me) % N)
    plane = [c for c in far if topo.same_plane(topo.chip(R), topo.chip(c))]
    mate = [c for c in far if topo.mates(topo.chip(R), topo.chip(c))]
    diag = [c for c in far if c not in plane and c not in mate]
    others = [c for c in topo.cores_of(R) if c != R]
    owners = [c for c in others if all(topo.may_write(c, d) for d in far)]
    c1 = [c for c in owners if topo.die(c) == topo.die(R)][0]
    c2 = [c for c in owners if topo.die(c) != topo.die(R)][0]
    ha, hb = [c for c in others if c not in owners and topo.die(c) != topo.die(R)][:2]
    return diag + mate + plane, c1, c2, ha, hb


def dst(c, topo):
    rid, pid, _ = topo.addr(c)
    return DstId(rid=rid, pnc=pid)


def copy_to(cores, src, dsts, mask, sem, topo):
    return RemoteDMATransfer(dst_ids=[dst(c, topo) for c in cores], dma_engine_mask=mask, remote_sem=sem, srcs=[src], dsts=dsts)


def engine_sets(R, near, far, topo):
    off = topo.engines(R, far)
    return off, [e for e in topo.engines(R, near) if e not in off]


def helper_program(g, core, R, T, topo):
    dests, c1, c2, ha, hb = roads(R, T, topo)
    if core not in (c1, c2, ha, hb):
        return
    out = topo.engines(core, dests[-1])
    mask, ne = bits_of(out), len(out)
    off, inner = engine_sets(R, core, dests[0], topo)
    codes = core in (c1, ha)
    mine = [0, 1, 2] if core in (c1, c2) else [3, 4]
    g.wait_ge(T.sem.hpl, len(off) if codes else len(inner))
    if codes:
        src = T.hq[:, 0:NBIT].bitcast(dt.uint8)
        ds = [T.pc[:, A0 + NBIT * j:A0 + NBIT * (j + 1)].bitcast(dt.uint8) for j in mine]
    else:
        src = T.hqz[:, 0:NBIT]
        ds = [T.pz[:, A0 + NBIT * j:A0 + NBIT * (j + 1)] for j in mine]
    g.remote_dma_fused([copy_to([dests[j] for j in mine], src, ds, mask, T.sem.pls, topo)], local_sem=T.sem.ls)
    total = ne
    if core in (ha, hb):
        j = 3 if core == ha else 4
        sem = T.sem["tb%d" % T.rank_of(R)]
        rid, pid, _ = topo.addr(dests[j])
        g.wait_ge(T.sem.hzs, len(inner))
        g.remote_dma(T["tz%d" % j][:, 0:K], T.hz[:, 0:K], sem, T.sem.ls, pid, rid, mask)
        g.wait_ge(T.sem.hcs, len(inner))
        g.remote_dma(T["tc%d" % j][:, 0:K].bitcast(dt.uint8), T.hc[:, 0:K].bitcast(dt.uint8), sem, T.sem.ls, pid, rid, mask)
        total += 2 * ne
    g.wait_ge(T.sem.ls, total)


def rank_program(g, core, T, topo):
    rank = T.rank_of(core)
    if rank is None:
        for R in T.cores:
            if topo.chip(R) == topo.chip(core):
                helper_program(g, core, R, T, topo)
        return
    dests, c1, c2, ha, hb = roads(core, T, topo)
    slot_q = [[T.rank_of(c) for c in T.cores if c != core and roads(c, T, topo)[0][j] == core][0] for j in range(N - 1)] + [rank]
    off, inner = engine_sets(core, ha, dests[0], topo)

    queue = {"v": g.vector, "s": g.scalar, "t": g.tensor, "y": g.sync, "g": g}
    own_sem = {"v": "sv", "s": "ss", "t": "st"}
    count = {"v": 0, "s": 0, "t": 0}
    seen = {}

    def need(q, sem, val):
        if seen.get((q, sem), 0) < val:
            seen[(q, sem)] = val
            queue[q].wait_ge(T.sem[sem], val)

    def done(q, ins):
        ins.then_inc(T.sem[own_sem[q]], 1)
        count[q] += 1
        return (own_sem[q], count[q])

    COPY = ActivationFunctionType.Copy

    def move(q, out, in_, after):
        for s, v in after:
            need(q, s, v)
        if q == "v":
            return done("v", g.vector.tensor_copy(out, in_))
        return done("s", g.scalar.activation(out, in_, COPY))

    def quantise(out, scales, in_, after):
        for s, v in after:
            need("v", s, v)
        return done("v", g.vector.quantize_mx(out, scales, in_))

    g.sync.dma_start(T.hpt[:, 4 * ZL:4 * (ZL + NBIT)], T.hp[:, 0:4 * NBIT]).then_inc(T.sem.ldh, 16)
    g.sync.dma_start(T.et[:, :], T.e[:, :]).then_inc(T.sem.lde, 16)
    g.sync.dma_start(T.xs[:, :, :], T.x[:, :]).then_inc(T.sem.ldx, 16)
    g.sync.dma_start(T.qwt[:, :], T.qw[:, :]).then_inc(T.sem.ldw, 16)

    z = done("v", g.vector.memset(T.hpt[:, 4 * (ZL + NBIT):4 * (ZL + 128)], 0.0))
    half = done("v", g.vector.memset(T.coef[:, :], 0.5))
    b0 = done("v", g.vector.memset(T.bf[:, :], 0.0))
    done("v", g.vector.memset(T.hpt[:, 0:4 * ZL], 0.0))
    zz = done("v", g.vector.memset(T.zt[:, :], 0.0))
    qh = quantise(T.hq[:, :], T.hqz[:, :], T.hpt[:, 4 * ZL:4 * (ZL + 128)], [("ldh", 16), z])
    quantise(T.pc[:, 0:A0], T.pz[:, 0:A0], T.zt[:, :], [zz])
    quantise(T.pc[:, Z1:Z1 + 128], T.pz[:, Z1:Z1 + 128], T.zt[:, :], [])
    quantise(T.oc[:, :], T.oz[:, :], T.hpt[:, :], [])
    half = done("v", g.vector.memset(T.coef[:, 0:3 * NR:NBIT], 0.0))
    qe = quantise(T.ec[:, :], T.ez[:, :], T.et[:, :], [("lde", 16)])
    cp = []
    for k in range(8):
        cp.append(move("s" if k < 3 else "v", T.xrep[:, :, 64 * k:64 * k + 64], T.xs[:, :, :], [("ldx", 16)]))
    qw = quantise(T.wc[:, :], T.wz[:, :], T.qwt[:, :], [("ldw", 16)])
    qx = [quantise(T.xc[:, 128 * i:128 * i + 128], T.xz[:, 128 * i:128 * i + 128], T.xrep[:, i, :], [cp[2], cp[7]]) for i in range(NC)]
    need("y", *qh)
    g.sync.dma_start(T.pc[:, GAP:Z1].bitcast(dt.uint8), T.hq[:, NBIT:2 * NBIT].bitcast(dt.uint8)).then_inc(T.sem.gap, 16)
    g.sync.dma_start(T.pz[:, GAP:Z1], T.hqz[:, NBIT:2 * NBIT]).then_inc(T.sem.gap, 16)

    need("g", *qh)
    pl = T.hq[:, 0:NBIT].bitcast(dt.uint8)
    g.remote_dma_fused([copy_to([c1, ha], pl, [pl, pl], bits_of(off), T.sem.hpl, topo)], local_sem=T.sem.ls)
    pl = T.hqz[:, 0:NBIT]
    g.remote_dma_fused([copy_to([c2, hb], pl, [pl, pl], bits_of(inner), T.sem.hpl, topo)], local_sem=T.sem.ls)
    need("g", *qe)
    total = len(off) + len(inner)
    for src, far, near, sem, codes in ((T.ez[:, 0:K], "tz", T.hz[:, 0:K], T.sem.hzs, False), (T.ec[:, 0:K], "tc", T.hc[:, 0:K], T.sem.hcs, True)):
        fars = [T["%s%d" % (far, j)][:, 0:K] for j in range(3)]
        if codes:
            src, near, fars = src.bitcast(dt.uint8), near.bitcast(dt.uint8), [d.bitcast(dt.uint8) for d in fars]
        g.remote_dma_fused([copy_to(dests[:3], src, fars, bits_of(off), T.sem["tb%d" % rank], topo),
                            copy_to([ha, hb], src, [near, near], bits_of(inner), sem, topo)], local_sem=T.sem.ls)
        total += len(off) + len(inner)

    free = [None] * BANKS
    unit = [0]

    def bank():
        b = unit[0] % BANKS
        unit[0] += 1
        if free[b] is not None:
            need("t", *free[b])
        return b

    def products(cd, sc_, after):
        res = []
        for s, v in after:
            need("t", s, v)
        for o in range(O):
            b = bank()
            m = done("t", g.tensor.matmul_mx(T["pb%d" % b][:, 0:K], T.wc[:, 128 * o:128 * o + 128], T.wz[:, 128 * o:128 * o + 128],
                                             cd[:, 0:K], sc_[:, 0:K], True, True))
            res.append((b, m))
        return res

    def drain(q, slot, o, bm):
        b, m = bm
        a = (slot * O + o) * K
        free[b] = move(q, T.pr[:, a:a + K], T["pb%d" % b][:, 0:K], [m])
        return free[b]

    def pick(q, slot, o, after):
        r = slot_q[slot]
        a, y = (slot * O + o) * K, (r * O + o) * TOK
        return move(q, T.yo[:, y:y + TOK], T.pr[:, a:a + K].indirect(T.li[:, NC * r:NC * r + NC]), after)

    nst = [0]

    def keep(out, in_, after):
        for s, v in after:
            need("y", s, v)
        g.sync.dma_start(out, in_).then_inc(T.sem.yst, 16)
        nst[0] += 1

    def store(slot, o0, o1, after):
        y = (slot_q[slot] * O) * TOK
        keep(T.y[:, y + o0 * TOK:y + o1 * TOK], T.yo[:, y + o0 * TOK:y + o1 * TOK], after)

    def bucket_products(lo, hi, cd, sc_, at, step):
        b = bank()
        for i in range(lo, hi):
            a = at - step * (i - lo)
            m = done("t", g.tensor.matmul_mx(T["pb%d" % b][:, 0:128], T.xc[:, 128 * i:128 * i + 128], T.xz[:, 128 * i:128 * i + 128],
                                             cd[:, a:a + 128], sc_[:, a:a + 128], i == lo, i == hi - 1))
        return b, m

    def numbers(bm, bits, out, n):
        b, m = bm
        need("v", *m)
        free[b] = done("v", g.vector.tensor_scalar(bits, T["pb%d" % b][:, 0:n], 0.0, 128.0, AluOpType.is_gt, AluOpType.mult))
        need("v", *free[b])
        need("v", *half)
        return done("v", g.vector.tensor_tensor_scan(out, T.coef[:, 0:n], bits, 0.0, AluOpType.mult, AluOpType.add))

    own = N - 1
    bm = products(T.ec, T.ez, [qe, qw])
    dr = [drain("s", own, o, bm[o]) for o in range(O)]
    need("t", *qx[-1])
    s = numbers(bucket_products(0, NC, T.oc, T.oz, ZL, NBIT), T.obits[:, :], T.osc[:, :], NC * NBIT)
    li = {own: move("v", T.li[:, NC * rank:NC * rank + NC], T.osc[:, NBIT - 1:NC * NBIT:NBIT], [s])}
    store(own, 0, O, [pick("s", own, o, [dr[o], li[own]]) for o in range(O)])

    need("t", "gap", 32)
    need("t", "pls", 2 * len(off) * (N - 1))
    groups = [bucket_products(lo, hi, T.pc, T.pz, A0, NR) for lo, hi in GROUPS]
    scans = [numbers(groups[k], T.bits[:, NR * lo:NR * hi], T.sc[:, NR * lo:NR * hi], NR * (hi - lo)) for k, (lo, hi) in enumerate(GROUPS)]

    def make_list(slot):
        r = slot_q[slot]
        li[slot] = move("v", T.li[:, NC * r:NC * r + NC], T.sc[:, NBIT * slot + NBIT - 1:NC * NR:NR], [scans[-1]])

    pm, dr = {}, {}

    def fetch(slot):
        pm[slot] = products(T["tc%d" % slot], T["tz%d" % slot], [("tb%d" % slot_q[slot], 2 * len(off))])

    make_list(0)
    make_list(1)
    fetch(0)
    for o in range(O):
        dr[0, o] = drain("s", 0, o, pm[0][o])
    last = N - 2
    for slot in range(N - 1):
        nxt = slot + 1
        if nxt <= last:
            fetch(nxt)
        p0 = pick("v", slot, 0, [dr[slot, 0], li[slot]])
        if nxt <= last:
            dr[nxt, 0] = drain("v", nxt, 0, pm[nxt][0])
        p1 = pick("s", slot, 1, [dr[slot, 1], li[slot]])
        if nxt <= last:
            dr[nxt, 1] = drain("s", nxt, 1, pm[nxt][1])
        p2 = pick("v", slot, 2, [dr[slot, 2]])
        if nxt <= last:
            dr[nxt, 2] = drain("s", nxt, 2, pm[nxt][2])
        if slot < last:
            if nxt < last:
                make_list(nxt + 1)
            store(slot, 0, O, [p0, p1, p2])
        else:
            store(slot, 0, 2, [p0, p1])
            store(slot, 2, O, [p2])

    need("v", *b0)
    h = NC * N // 2
    move("v", T.bf[0:32, 0:h], T.li[0:32, 0:h], [li[N - 2]])
    f = move("v", T.bf[0:32, 32:32 + h], T.li[0:32, h:2 * h], [])
    need("v", *f)
    tr = done("v", g.vector.transpose(T.bt[0:32, :], T.bf[0:32, :]))
    keep(T.bk[0:N // 2, :], T.bt[0:h, 0:16], [tr])
    keep(T.bk[N // 2:N, :], T.bt[0:h, 32:48], [])

    need("y", "yst", 16 * nst[0])
    need("g", "ls", total)
    for q in ("v", "s", "t"):
        need("g", own_sem[q], count[q])
